import numpy as np
import ml_dtypes


def mxq(x, axis, fmt="e4m3"):
    dtype, down = {"e4m3": (ml_dtypes.float8_e4m3fn, 7), "e5m2": (ml_dtypes.float8_e5m2, 14)}[fmt]
    v = np.moveaxis(np.asarray(x, np.float32).astype(ml_dtypes.bfloat16).astype(np.float64), axis, -1)
    blocks = v.reshape(v.shape[:-1] + (-1, 32))
    amax = np.abs(blocks).max(-1, keepdims=True)
    byte = np.maximum(np.where(amax > 0, np.frexp(amax)[1] - 1 + 127, 0) - down, 1)
    scale = np.exp2(byte - 127.0)
    codes = (blocks / scale).astype(np.float32).astype(dtype).astype(np.float64)
    return np.moveaxis((codes * scale).reshape(v.shape), -1, axis)


WIDE = False


def mx_kscale(k):
    if not WIDE:
        return np.ones(k)
    levels = np.array([10, -10, 5, -5, 0])
    if k % 512:
        return np.exp2(np.random.permutation(np.resize(levels, k // 32))).repeat(32)
    a = np.empty((k // 512, 16))
    for p in range(k // 512):
        a[p, :8] = np.random.permutation(np.resize(levels, 8))
        for g in range(8):
            far = levels[np.abs(levels - a[p, g]) >= 10]
            a[p, g + 8] = far[np.random.randint(len(far))]
    return np.exp2(a.ravel()).repeat(32)


BF16 = ml_dtypes.bfloat16


def bf(x):
    return np.asarray(x, np.float32).astype(BF16)


def f64(x):
    return np.asarray(x).astype(np.float64)


E2M1 = np.array([0.0, 0.5, 1.0, 1.5, 2.0, 3.0, 4.0, 6.0, -0.0, -0.5, -1.0, -1.5, -2.0, -3.0, -4.0, -6.0])


def pack_weight(w, fmt):
    k, n = w.shape
    w = f64(bf(w)).reshape(k // 32, 32, n)
    amax = np.abs(w).max(1)
    if fmt == "e4m3":
        byte = np.frexp(amax)[1] - 1 + 127 - 7
    else:
        mant, ex = np.frexp(amax / 6.0)
        byte = np.where(mant > 0.5, ex, ex - 1) + 127
    byte = np.clip(np.where(amax > 0, byte, 1), 1, 254)
    scaled = (w * np.exp2(127.0 - byte)[:, None, :]).reshape(k, n).astype(np.float32)
    by_word = np.ascontiguousarray(scaled.reshape(k // 512, 128, 4, n).transpose(0, 1, 3, 2))
    if fmt == "e4m3":
        words = by_word.astype(ml_dtypes.float8_e4m3fn).view(np.uint8)
    else:
        c = by_word.astype(ml_dtypes.float4_e2m1fn).view(np.uint8) & 0xF
        words = c[..., 0::2] | (c[..., 1::2] << 4)
    return np.ascontiguousarray(words), np.ascontiguousarray(byte.astype(np.uint8).reshape(k // 512, 16, n))


def unpack_weight(words, scales, fmt):
    g, p, n, _ = words.shape
    if fmt == "e4m3":
        vals = np.ascontiguousarray(words).view(ml_dtypes.float8_e4m3fn).astype(np.float64)
    else:
        nib = np.empty((g, p, n, 4), np.uint8)
        nib[..., 0::2] = words & 0xF
        nib[..., 1::2] = words >> 4
        vals = E2M1[nib]
    vals = vals * np.repeat(np.exp2(scales.astype(np.float64) - 127.0), 8, axis=1)[..., None]
    return vals.transpose(0, 1, 3, 2).reshape(g * 512, n)
def pack4(w):
    words, scales = pack_weight(w, "e2m1")
    return words.reshape(words.shape[0], 128, -1), scales


def unpack4(words, scales):
    return unpack_weight(words.reshape(words.shape[0], 128, -1, 2), scales, "e2m1")


def planes(Y):
    n, m = Y.shape
    b = f64(bf(Y)).reshape(n // 32, 32, m)
    amax = np.abs(b).max(1)
    byte = np.clip(np.where(amax > 0, np.frexp(amax)[1] - 1 + 127 - 7, 1), 1, 254)
    codes = (b * np.exp2(127.0 - byte)[:, None, :]).reshape(n, m).astype(np.float32).astype(ml_dtypes.float8_e4m3fn).view(np.uint8)
    words = codes.reshape(n // 512, 128, 4, m).transpose(0, 1, 3, 2)
    return np.ascontiguousarray(words), np.ascontiguousarray(byte.astype(np.uint8).reshape(n // 512, 16, m))


N, D, F, H = 1024, 1024, 1024, 2
HEAD_GAIN = np.array([2.0, 1.0])
P_HIT = 0.3


def softplus(v):
    return np.maximum(v, 0.0) + np.log(1.0 + np.exp(-np.abs(v)))


def setup_inputs():
    r, t = mx_kscale(D), mx_kscale(F)
    x = bf(np.random.standard_normal((N, D)))
    xbar = bf(np.random.standard_normal((N, D)))
    u = bf(np.random.uniform(0.0, 1.0, (N, D)))
    s = bf((1.0 + 0.1 * np.random.standard_normal(D)) * r)
    we_words, we_scales = pack4(np.random.standard_normal((D, F)) / np.sqrt(D) / r[:, None])
    return {"x": x,
            "xbar": xbar,
            "u": u,
            "s": s,
            "we_words": we_words,
            "we_scales": we_scales,
            "g": bf((1.0 + 0.1 * np.random.standard_normal(F)) * t),
            "wh": bf(np.random.standard_normal((H, F, D)) * HEAD_GAIN[:, None, None] / np.sqrt(F) / t[None, :, None])}


def corrupt(x, xbar, u, s):
    hit = u < P_HIT
    m = np.where(hit, 1.0, 0.0)
    xt = s[None, :] * np.where(hit, xbar, x)
    return m, xt


def encode(xt, we, g):
    return g[None, :] * np.tanh(mxq(xt, 1, "e4m3") @ we)


def core(x, xbar, u, s, we_words, we_scales, g, wh):
    x, xbar, u, s, g, wh = f64(x), f64(xbar), f64(u), f64(s), f64(g), f64(wh)
    we = unpack4(we_words, we_scales)
    m, xt = corrupt(x, xbar, u, s)
    h = encode(xt, we, g)
    hq = mxq(h, 1, "e4m3")
    whq = mxq(wh, 1, "e4m3")
    a = hq @ whq[0]
    rec = hq @ whq[1]
    return softplus(a) - m * a + 2.0 * np.square(rec - x)


def reference(x, xbar, u, s, we_words, we_scales, g, wh):
    R_out = core(x, xbar, u, s, we_words, we_scales, g, wh)
    words, scales = planes(R_out.T)
    return R_out, words, scales

import math
from contextlib import ExitStack

import concourse.mybir as mybir
from concourse.masks import make_identity

F32 = mybir.dt.float32
BF16 = mybir.dt.bfloat16
I32 = mybir.dt.int32
U32 = mybir.dt.uint32
U8 = mybir.dt.uint8
FP8X4 = mybir.dt.float8_e4m3fn_x4
FP4X4 = mybir.dt.float4_e2m1fn_x4
ALU = mybir.AluOpType
ACT = mybir.ActivationFunctionType

P = 128
TILES = 8
W = 1024
FLOPS = 3 * 2 * 1024 ** 3
P_HIT = 0.3
GMODE = "DDDVVVVV"
NMODE = "VVVVVVVV"
RMODE = "DDDDAAVV"
CMODE = "AAAAAAAA"
OMODE = "VVVVVVVV"
WMODE = "AAAAAAPPPPPPPPPP"
TINY = 2.0 ** -60
ORDER = [
    ("lu", 0), ("lx", 0), ("n", 0), ("lb", 0), ("lu", 1), ("lb", 1), ("m", 0), ("t2", 0), ("lw", 0, 0), ("lx", 1), ("t1", 0), ("n", 1), ("cw", 0, 0),
    ("m", 1), ("lu", 2), ("sel", 0), ("ls",), ("t1", 1), ("t2", 1), ("lw", 0, 1), ("n", 2), ("lb", 2), ("cw", 0, 1), ("T", 0), ("cw", 0, 2), ("ss",),
    ("sel", 1), ("T", 1), ("xt", 0), ("m", 2), ("lx", 2), ("lwe",), ("qw", 0, 0), ("qx", 0), ("xt", 1), ("W", 1, 2), ("lsm",), ("t1", 2), ("W", 1, 3),
    ("lu", 3), ("lb", 3), ("cw", 0, 3), ("t2", 2), ("cw", 1, 0), ("cw", 1, 1), ("qw", 0, 1), ("swc",), ("sws",), ("lx", 3), ("lu", 4), ("cw", 1, 2),
    ("S", 0, 0), ("sel", 2), ("cw", 1, 3), ("S", 0, 1), ("th", 0, 0), ("lx", 4), ("sg",), ("qx", 1), ("n", 3), ("m", 3), ("qw", 1, 0), ("T", 2),
    ("S", 1, 0), ("t1", 3), ("t2", 3), ("lw", 1, 0), ("xt", 2), ("lu", 5), ("sel", 3), ("S", 1, 1), ("th", 0, 1), ("qx", 2), ("lb", 4), ("gs", 0, 0),
    ("T", 3), ("gs", 0, 1), ("th", 1, 0), ("ch", 0), ("gs", 1, 0), ("th", 1, 1), ("S", 2, 0), ("S", 2, 1), ("lb", 5), ("th", 2, 0), ("n", 4),
    ("m", 4), ("qw", 1, 1), ("t2", 4), ("xt", 3), ("W", 2, 0), ("lx", 5), ("th", 2, 1), ("gs", 1, 1), ("n", 5), ("qh", 0), ("t1", 4), ("qx", 3),
    ("A", 0, 0), ("m", 5), ("lu", 6), ("A", 0, 1), ("gs", 2, 0), ("lx", 6), ("t2", 5), ("t1", 5), ("gs", 2, 1), ("S", 3, 0), ("sel", 4), ("ch", 1),
    ("sel", 5), ("lu", 7), ("W", 2, 1), ("lw", 1, 1), ("T", 4), ("n", 6), ("z", 0, 0), ("z", 0, 1), ("qh", 1), ("cw", 2, 0), ("lb", 6), ("cw", 2, 1),
    ("xt", 4), ("m", 6), ("lx", 7), ("S", 3, 1), ("ch", 2), ("T", 5), ("A", 1, 0), ("W", 2, 2), ("th", 3, 0), ("t2", 6), ("sig", 0), ("th", 3, 1),
    ("qx", 4), ("n", 7), ("qh", 2), ("xt", 5), ("S", 4, 0), ("S", 4, 1), ("z", 1, 0), ("A", 1, 1), ("t1", 6), ("cw", 2, 2), ("qw", 2, 0), ("sel", 6),
    ("qx", 5), ("th", 4, 0), ("z", 1, 1), ("W", 2, 3), ("A", 2, 0), ("th", 4, 1), ("T", 6), ("A", 2, 1), ("g", 3), ("t2", 7), ("S", 5, 0), ("ln", 0),
    ("W", 3, 0), ("xt", 6), ("S", 5, 1), ("z", 2, 0), ("z", 2, 1), ("m", 7), ("W", 3, 1), ("qh", 3), ("lb", 7), ("cw", 2, 3), ("qw", 2, 1),
    ("A", 3, 0), ("sig", 1), ("th", 5, 0), ("g", 4), ("t1", 7), ("qx", 6), ("mn", 0), ("z", 3, 0), ("qh", 4), ("th", 5, 1), ("sel", 7), ("A", 3, 1),
    ("W", 3, 2), ("cw", 3, 0), ("W", 3, 3), ("S", 6, 0), ("S", 6, 1), ("z", 3, 1), ("cw", 3, 1), ("qw", 3, 0), ("T", 7), ("g", 5), ("sig", 2),
    ("cw", 3, 2), ("cw", 3, 3), ("th", 6, 0), ("R", 0, 0), ("qw", 3, 1), ("xt", 7), ("sig", 3), ("dl", 0, 0), ("A", 4, 0), ("th", 6, 1), ("ln", 1),
    ("z", 4, 0), ("R", 0, 1), ("dl", 0, 1), ("R", 1, 0), ("R", 1, 1), ("dl", 1, 0), ("g", 6), ("A", 4, 1), ("ln", 2), ("dl", 1, 1), ("R", 2, 0),
    ("dl", 2, 0), ("R", 2, 1), ("qh", 5), ("R", 3, 0), ("R", 3, 1), ("dl", 2, 1), ("qx", 7), ("sq", 0), ("A", 5, 0), ("z", 4, 1), ("z", 5, 0),
    ("R", 4, 0), ("S", 7, 0), ("ln", 3), ("qh", 6), ("out", 0, 2), ("dl", 3, 0), ("S", 7, 1), ("sig", 4), ("A", 5, 1), ("sq", 1), ("z", 5, 1),
    ("mn", 1), ("dl", 3, 1), ("so", 0, 2), ("R", 4, 1), ("out", 1, 2), ("A", 6, 0), ("th", 7, 0), ("RT", 0, 0), ("RT", 0, 1), ("th", 7, 1),
    ("R", 5, 0), ("sig", 5), ("dl", 4, 0), ("cr", 0, 0), ("g", 7), ("z", 6, 0), ("sq", 2), ("R", 5, 1), ("dl", 4, 1), ("RT", 1, 0), ("qh", 7),
    ("so", 1, 2), ("A", 6, 1), ("A", 7, 0), ("mn", 2), ("A", 7, 1), ("cr", 0, 1), ("R", 6, 0), ("z", 6, 1), ("sq", 3), ("R", 6, 1), ("z", 7, 0),
    ("z", 7, 1), ("cr", 1, 0), ("sq", 4), ("out", 2, 2), ("mn", 3), ("sig", 6), ("dl", 5, 0), ("qr", 0, 0), ("qr", 0, 1), ("dl", 5, 1), ("R", 7, 0),
    ("out", 3, 2), ("sig", 7), ("RT", 1, 1), ("ln", 4), ("cr", 1, 1), ("ln", 5), ("ln", 6), ("dl", 6, 0), ("RT", 2, 0), ("mn", 4), ("dl", 6, 1),
    ("sq", 5), ("R", 7, 1), ("ln", 7), ("RT", 2, 1), ("mn", 5), ("out", 4, 2), ("dl", 7, 0), ("RT", 3, 0), ("qr", 1, 0), ("qr", 1, 1), ("rc", 4, 2),
    ("dl", 7, 1), ("RT", 3, 1), ("sq", 6), ("RT", 4, 2), ("so", 2, 2), ("out", 5, 2), ("cr", 2, 0), ("mn", 6), ("sq", 7), ("qr", 2, 0), ("rc", 5, 2),
    ("mn", 7), ("cr", 2, 1), ("out", 6, 2), ("cr", 3, 0), ("out", 7, 0), ("so", 3, 2), ("qr", 2, 1), ("RT", 5, 2), ("so", 4, 2), ("cr", 3, 1),
    ("sc", 0), ("rc", 6, 2), ("cr", 4, 2), ("rc", 7, 0), ("so", 5, 2), ("RT", 6, 2), ("qr", 3, 0), ("qr", 3, 1), ("cr", 5, 2), ("so", 6, 2),
    ("out", 7, 1), ("qr", 4, 0), ("qr", 4, 1), ("cr", 6, 2), ("RT", 7, 0), ("rc", 7, 1), ("qr", 5, 0), ("qr", 5, 1), ("qr", 6, 0), ("so", 7, 0),
    ("qr", 6, 1), ("sc", 1), ("RT", 7, 1), ("cr", 7, 0), ("cr", 7, 1), ("qr", 7, 0), ("so", 7, 1), ("sc", 2), ("qr", 7, 1), ("sc", 3, 0),
    ("sc", 3, 1), ("ssc",),
]


def tile_vimemaskandfeaturepretextloss_x2_kernel(tc, x, xbar, u, s, we_words, we_scales, g, wh, out_0, out_1, out_2):
    nc = tc.nc
    with ExitStack() as ctx:
        keep = ctx.enter_context(tc.tile_pool(name="keep", bufs=1))
        ring = ctx.enter_context(tc.tile_pool(name="ring", bufs=2))
        psum = ctx.enter_context(tc.psum_pool(name="psum", bufs=1))
        ctx.enter_context(tc.manual_schedule())

        free_banks = list(range(8))
        held = dict()

        def bank(key, shape, dtype):
            held[key] = free_banks.pop(0)
            return psum.tile(shape, dtype, name="bank%d" % held[key], tag="bank%d" % held[key])

        def release(key):
            free_banks.append(held[key])

        xs, us, xbs, m2s, n2s, sels, xtps, xtbs, xqs, s1s, ths, hbs, hqs = [dict() for k in range(13)]
        zs, abanks, rbanks, dls, tbanks, rbs, wraws, wbs, wqs, wbanks = [dict() for k in range(10)]

        def load_u(i):
            us[i] = ring.tile([P, W], BF16, name="u", tag="u", bufs=3)
            nc.sync.dma_start(out=us[i][:], in_=u[P * i : P * (i + 1), :])

        def load_xb(i):
            xbs[i] = ring.tile([P, W], BF16, name="xb", tag="xb", bufs=3)
            nc.sync.dma_start(out=xbs[i][:], in_=xbar[P * i : P * (i + 1), :])

        def load_x(i):
            xs[i] = keep.tile([P, W], BF16, name="x%d" % i)
            nc.sync.dma_start(out=xs[i][:], in_=x[P * i : P * (i + 1), :])

        def load_wh(h, f):
            k = 2 * h + f
            wraws[k] = keep.tile([P, 4, W], BF16, name="whraw%d" % k, tag="big%d" % (4 + k))
            src = wh[h, 512 * f : 512 * (f + 1), :].rearrange("(q t e) d -> e q t d", t=4, e=4)
            for e in range(4):
                nc.sync.dma_start(out=wraws[k][e:P:4, :, :], in_=src[e])

        warm = keep.tile([P, 2], F32, name="warm")
        nc.vector.memset(warm[:], 0.0)
        sraw = ring.tile([P, 2, W], U8, name="sraw", tag="dl", bufs=8, align_bytes=64)
        nc.vector.memset(sraw[:].bitcast(I32), 0)
        grow = keep.tile([P, P], BF16, name="grow")
        nc.vector.memset(grow[:], 0.0)
        nc.scalar.activation(out=warm[:, 1:2], in_=warm[:, 0:1], func=ACT.Sigmoid)
        ident_f = keep.tile([P, P], F32, name="ident_f")
        make_identity(nc, ident_f[:])
        ident_b = keep.tile([P, P], BF16, name="ident_b")
        make_identity(nc, ident_b[:])
        s4 = keep.tile([P, 2, 4], BF16, name="s4")
        weraw = ring.tile([P, 2, 2 * W], U8, name="weraw", tag="dl", bufs=8, align_bytes=64)

        def load_small():
            for q in range(4):
                nc.sync.dma_start(
                    out=sraw[32 * q : 32 * q + 4, :, :].bitcast(I32),
                    in_=we_scales[:, 4 * q : 4 * q + 4, :].rearrange("G r n -> r G n").bitcast(I32),
                )
            for f in range(2):
                nc.sync.dma_start(
                    out=grow[4 * f : 4 * f + 4, :].rearrange("t (q e) -> t q e", e=4),
                    in_=g[512 * f : 512 * (f + 1)].rearrange("(q t e) -> t q e", t=4, e=4),
                )

        def load_s():
            nc.sync.dma_start(out=s4[:], in_=s.rearrange("(G p t) -> p G t", G=2, t=4))

        def load_we():
            nc.sync.dma_start(out=weraw[:].bitcast(I32), in_=we_words.rearrange("G p b -> p G b").bitcast(I32))

        s_half = keep.tile([P, 2, 4], BF16, name="s_half")
        g8 = keep.tile([P, 2, 4], BF16, name="g8")
        g32 = keep.tile([P, 8], F32, name="g32")
        hrs, hbanks = dict(), dict()
        we_c = keep.tile([P, 4, 4, 256], U8, name="we_c", align_bytes=64)
        we_s = keep.tile([P, 4, 4, P], U8, name="we_s", align_bytes=64)
        ocs = dict()
        osc = keep.tile([P, 2, W], U8, name="osc", align_bytes=64)

        def setup_s():
            nc.vector.tensor_scalar(out=s_half[:], in0=s4[:], scalar1=0.5, scalar2=None, op0=ALU.mult)

        def setup_g():
            gp = bank("g", [P, P], BF16)
            nc.tensor.transpose(gp[:], grow[:], ident_b[:])
            nc.scalar.copy(out=g8[:].rearrange("p f t -> p (f t)"), in_=gp[:, 0:8])
            nc.scalar.copy(out=g32[:], in_=gp[:, 0:8])
            release("g")

        def setup_we_scales():
            nc.vector.tensor_copy(
                out=we_s[:].bitcast(I32),
                in_=sraw[:].bitcast(I32).rearrange("p G (f q t) -> p (G f) t q", f=2, t=4),
            )

        def setup_we_codes():
            nc.vector.tensor_copy(
                out=we_c[:].bitcast(I32).rearrange("p k t (q h) -> p k t q h", h=2),
                in_=weraw[:].bitcast(I32).rearrange("p G (f q t h) -> p (G f) t q h", f=2, t=4, h=2),
            )

        def v_m2(i):
            m2s[i] = ring.tile([P, W], BF16, name="m2", tag="m2", bufs=6)
            nc.vector.tensor_scalar(out=m2s[i][:], in0=us[i][:], scalar1=P_HIT, scalar2=2.0, op0=ALU.is_lt, op1=ALU.mult)

        def v_n2(i):
            n2s[i] = ring.tile([P, W], BF16, name="n2", tag="n2")
            if NMODE[i] == "V":
                nc.vector.tensor_scalar(out=n2s[i][:], in0=us[i][:], scalar1=P_HIT, scalar2=2.0, op0=ALU.is_ge, op1=ALU.mult)
            else:
                nc.scalar.activation(out=n2s[i][:], in_=m2s[i][:], func=ACT.Identity, scale=-1.0, bias=2.0)

        def v_t1(i):
            sels[i] = ring.tile([P, W], BF16, name="sel", tag="sel")
            nc.vector.tensor_tensor(out=sels[i][:], in0=m2s[i][:], in1=xbs[i][:], op=ALU.mult)

        def v_t2(i):
            nc.vector.tensor_tensor(out=n2s[i][:], in0=n2s[i][:], in1=xs[i][:], op=ALU.mult)

        def v_sel(i):
            nc.vector.tensor_tensor(out=sels[i][:], in0=sels[i][:], in1=n2s[i][:], op=ALU.add)

        def pe_xt(i):
            xtps[i] = bank(("x", i), [P, 2, 2, P], F32)
            words = sels[i][:].bitcast(F32)
            for G in range(2):
                for v in range(2):
                    nc.tensor.transpose(xtps[i][:, v, G, :], words[:, 256 * G + v : 256 * (G + 1) : 2], ident_f[:])

        def v_xt(i):
            xtbs[i] = ring.tile([P, 2, P, 2, 2], BF16, name="xtb", tag="xtb", align_bytes=64)
            nc.vector.tensor_tensor(
                out=xtbs[i][:],
                in0=xtps[i][:].bitcast(BF16).rearrange("p v G (n e) -> p G n v e", e=2),
                in1=s_half[:].rearrange("p G (v e) -> p G v e", e=2).unsqueeze(2).to_broadcast([P, 2, P, 2, 2]),
                op=ALU.mult,
            )
            release(("x", i))

        def v_qx(i):
            c = ring.tile([P, 2 * P], U32, name="xq", tag="xq", align_bytes=64)
            sc = ring.tile([P, 2 * P], U8, name="xqs", tag="xqs", align_bytes=64)
            xqs[i] = (c, sc)
            nc.vector.quantize_mx(out=c[:].bitcast(FP8X4), scales=sc[:], in_=xtbs[i][:].rearrange("p G n v e -> p (G n v e)"))

        def pe_s1(i, f):
            s1s[i, f] = bank(("s", i, f), [P, 4, P], F32)
            c, sc = xqs[i]
            for t in range(4):
                for G in range(2):
                    nc.tensor.matmul_mx(
                        out=s1s[i, f][:, t, :],
                        lhsT=we_c[:, 2 * G + f, t, :].bitcast(FP4X4),
                        lhsT_scale=we_s[:, 2 * G + f, t, :],
                        rhs=c[:, P * G : P * (G + 1)].bitcast(FP8X4),
                        rhs_scale=sc[:, P * G : P * (G + 1)],
                        start=(G == 0),
                        stop=(G == 1),
                    )

        def a_tanh(i, f):
            if f == 0:
                ths[i] = ring.tile([P, 2, P, 4], F32, name="th", tag="th")
            if GMODE[i] in "VPH":
                nc.scalar.activation(out=ths[i][:, f, :, :], in_=s1s[i, f][:].rearrange("p t n -> p n t"), func=ACT.Tanh)
            else:
                nc.scalar.activation(out=ths[i][:, f, :, :].rearrange("p n t -> p (n t)"), in_=s1s[i, f][:].rearrange("p t n -> p (t n)"), func=ACT.Tanh)
            release(("s", i, f))

        def a_gs(i, f):
            if f == 0:
                hrs[i] = ring.tile([P, 2, 4, P], BF16, name="hr", tag="hr")
            for t in range(4):
                nc.scalar.activation(
                    out=hrs[i][:, f, t, :],
                    in_=ths[i][:, f, :, :].rearrange("p n t -> p (n t)")[:, P * t : P * (t + 1)],
                    func=ACT.Copy,
                    scale=g32[:, 4 * f + t : 4 * f + t + 1],
                )

        def pe_h(i):
            hbanks[i] = bank(("h", i), [P, 2, 512], BF16)
            for f in range(2):
                nc.tensor.matmul(out=hbanks[i][:, f, :], lhsT=ident_b[:], rhs=hrs[i][:, f, :, :].rearrange("p t n -> p n t"), start=True, stop=True)

        def a_ch(i):
            hbs[i] = ring.tile([P, 2, P, 4], BF16, name="hb", tag="hb", align_bytes=64)
            if GMODE[i] == "B":
                nc.scalar.copy(out=hbs[i][:].rearrange("p f n t -> p (f n t)"), in_=hbanks[i][:].rearrange("p f n -> p (f n)"))
                release(("h", i))
            else:
                nc.scalar.copy(
                    out=hbs[i][:].rearrange("p f (c i) t -> p f c t i", i=4), in_=hrs[i][:].rearrange("p f t (c i) -> p f c t i", i=4)
                )

        def v_g(i, part=2):
            if part != 1:
                hbs[i] = ring.tile([P, 2, P, 4], BF16, name="hb", tag="hb", align_bytes=64)
            fs = [slice(0, 1), slice(1, 2), slice(0, 2)][part]
            on_pool = GMODE[i] == "P" or (GMODE[i] == "H" and part == 1)
            eng = nc.gpsimd if on_pool else nc.vector
            eng.tensor_tensor(
                out=hbs[i][:, fs, :, :], in0=ths[i][:, fs, :, :], in1=g8[:, fs, :].unsqueeze(2).to_broadcast([P, 1 + part // 2, P, 4]), op=ALU.mult
            )

        def v_qh(i):
            c = keep.tile([P, 2 * P], U32, name="hq%d" % i, align_bytes=64)
            sc = keep.tile([P, 2 * P], U8, name="hqs%d" % i, align_bytes=64)
            hqs[i] = (c, sc)
            nc.vector.quantize_mx(out=c[:].bitcast(FP8X4), scales=sc[:], in_=hbs[i][:].rearrange("p f n t -> p (f n t)"))

        def pe_w(k, j):
            wbanks[k, j] = bank(("w", k, j), [P, 2, 512], BF16)
            for c in range(2):
                d0 = 256 * j + P * c
                nc.tensor.matmul(
                    out=wbanks[k, j][:, c, :],
                    lhsT=ident_b[:],
                    rhs=wraws[k][:, :, d0 : d0 + P].rearrange("p t d -> p d t"),
                    start=True,
                    stop=True,
                )

        def a_w(k, j):
            if j % 2 == 0:
                wbs[k, j // 2] = ring.tile([P, 2, W], BF16, name="wb", tag="wb", bufs=2, align_bytes=64)
            if WMODE[4 * k + j] == "P":
                nc.scalar.copy(out=wbs[k, j // 2][:, j % 2, :], in_=wbanks[k, j][:].rearrange("p c n -> p (c n)"))
                release(("w", k, j))
            else:
                nc.scalar.copy(
                    out=wbs[k, j // 2][:, j % 2, :].rearrange("p (c i t) -> p c t i", i=4, t=4),
                    in_=wraws[k][:, :, 256 * j : 256 * (j + 1)].rearrange("p t (c i) -> p c t i", i=4),
                )

        def w_half(k, dh):
            for j in (2 * dh, 2 * dh + 1):
                pe_w(k, j)
                a_w(k, j)

        def v_qw(k, dh):
            c = keep.tile([P, 512], U32, name="wq%d_%d" % (k, dh), align_bytes=64)
            sc = keep.tile([P, 512], U8, name="wqs%d_%d" % (k, dh), align_bytes=64)
            wqs[k, dh] = (c, sc)
            nc.vector.quantize_mx(out=c[:].bitcast(FP8X4), scales=sc[:], in_=wbs[k, dh][:].rearrange("p j n -> p (j n)"))

        def pe_s2(h, i, dh):
            acc = bank((h, i, dh), [P, 512], F32)
            c, sc = hqs[i]
            for f in range(2):
                wc, ws = wqs[2 * h + f, dh]
                nc.tensor.matmul_mx(
                    out=acc[:],
                    lhsT=c[:, P * f : P * (f + 1)].bitcast(FP8X4),
                    lhsT_scale=sc[:, P * f : P * (f + 1)],
                    rhs=wc[:].bitcast(FP8X4),
                    rhs_scale=ws[:],
                    start=(f == 0),
                    stop=(f == 1),
                )
            return acc

        def v_z(i, dh):
            if dh == 0:
                zs[i] = keep.tile([P, 2, W], F32, name="zs%d" % i, tag="big%d" % i)
            cols = slice(512 * dh, 512 * (dh + 1))
            nc.vector.scalar_tensor_tensor(
                out=zs[i][:, 0, cols], in0=m2s[i][:, cols], scalar=1.0, in1=abanks[i, dh][:], op0=ALU.subtract, op1=ALU.mult
            )
            release((0, i, dh))

        def a_sig(i):
            nc.scalar.activation(out=zs[i][:, 1, :], in_=zs[i][:, 0, :], func=ACT.Sigmoid)

        def v_dl(i, dh):
            if dh == 0:
                dls[i] = ring.tile([P, W], F32, name="dl", tag="dl", bufs=8, align_bytes=64)
            cols = slice(512 * dh, 512 * (dh + 1))
            nc.vector.tensor_tensor(out=dls[i][:, cols], in0=rbanks[i, dh][:], in1=xs[i][:, cols], op=ALU.subtract)
            release((1, i, dh))

        def a_sq(i):
            nc.scalar.activation(out=dls[i][:], in_=dls[i][:], func=ACT.Square, scale=math.sqrt(2.0))

        def a_ln(i):
            nc.scalar.activation(out=zs[i][:, 1, :], in_=zs[i][:, 1, :], func=ACT.Ln, bias=TINY)

        def v_min(i):
            nc.vector.tensor_tensor(out=zs[i][:, 0, :], in0=zs[i][:, 0, :], in1=zs[i][:, 1, :], op=ALU.min)

        def v_out(i, cols, eng):
            eng.tensor_tensor(out=zs[i][:, 1, cols], in0=dls[i][:, cols], in1=zs[i][:, 0, cols], op=ALU.subtract)

        def store_out(i, part):
            cols = [slice(0, 512), slice(512, W), slice(0, W)][part]
            nc.sync.dma_start(out=out_0[P * i : P * (i + 1), cols], in_=zs[i][:, 1, cols])

        rcs = dict()

        def cast_r(i, part):
            if part != 1:
                rcs[i] = ring.tile([P, W], BF16, name="rc", tag="rc")
            cols = [slice(0, 512), slice(512, W), slice(0, W)][part]
            dst = rcs[i][:, cols].rearrange("p (G v q e) -> p G v q e", v=2, q=P, e=2)
            src = zs[i][:, 1, cols].rearrange("p (G q v e) -> p G v q e", v=2, q=P, e=2)
            if RMODE[i] == "A":
                nc.scalar.copy(out=dst, in_=src)
            elif RMODE[i] == "P":
                for G in range(1 + part // 2):
                    nc.gpsimd.tensor_scalar(out=dst[:, G], in0=src[:, G], scalar1=1.0, scalar2=0.0, op0=ALU.mult, op1=ALU.add)
            else:
                nc.vector.tensor_copy(out=dst, in_=src)

        def pe_rt(i, part):
            if RMODE[i] == "D":
                tbanks[i, part] = bank(("r", i, part), [P, 4, P], F32)
                for t in range(4):
                    nc.tensor.transpose(tbanks[i, part][:, t, :], zs[i][:, 1, 512 * part + t : 512 * (part + 1) : 4], ident_f[:])
            else:
                tbanks[i, part] = bank(("r", i, part), [P, 2, 2, P], F32)
                words = rcs[i][:].bitcast(F32)
                for G in [[0], [1], [0, 1]][part]:
                    for v in range(2):
                        nc.tensor.transpose(tbanks[i, part][:, G, v, :], words[:, 256 * G + P * v : 256 * G + P * (v + 1)], ident_f[:])

        def a_rt(i, part):
            if part != 1:
                rbs[i] = ring.tile([P, 2, P, 4], BF16, name="rb", tag="rb", align_bytes=64)
            if RMODE[i] == "D":
                dst, src = rbs[i][:, part, :, :], tbanks[i, part][:].rearrange("p t n -> p n t")
            else:
                Gs = [slice(0, 1), slice(1, 2), slice(0, 2)][part]
                dst, src = rbs[i][:, Gs, :, :].bitcast(F32), tbanks[i, part][:, Gs, :, :].rearrange("p G v n -> p G n v")
            if CMODE[i] == "A":
                nc.scalar.copy(out=dst, in_=src)
            else:
                nc.vector.tensor_copy(out=dst, in_=src)
            release(("r", i, part))

        def v_qr(i, G):
            if i % 2 == 0 and G == 0:
                ocs[i // 2] = keep.tile([P, 2, 2 * P], U32, name="oc%d" % (i // 2), align_bytes=64)
            nc.vector.quantize_mx(
                out=ocs[i // 2][:, G, P * (i % 2) : P * (i % 2 + 1)].bitcast(FP8X4),
                scales=osc[:, G, P * i : P * (i + 1)],
                in_=rbs[i][:, G, :, :].rearrange("p n t -> p (n t)"),
            )

        def store_codes(j, part=2):
            lo, hi = [(0, P), (P, 2 * P), (0, 2 * P)][part]
            nc.sync.dma_start(
                out=out_1.rearrange("G p n t -> p G (n t)").bitcast(I32)[:, :, 2 * P * j + lo : 2 * P * j + hi],
                in_=ocs[j][:, :, lo:hi].bitcast(I32),
            )

        def store_scales():
            for q in range(4):
                eng = nc.sync if q % 2 else nc.scalar
                eng.dma_start(
                    out=out_2[:, 4 * q : 4 * q + 4, :].rearrange("G r n -> r G n").bitcast(I32),
                    in_=osc[32 * q : 32 * q + 4, :, :].bitcast(I32),
                )

        def ok(i):
            return 0 <= i < TILES

        def rec(j, dh):
            rbanks[j, dh] = pe_s2(1, j, dh)

        def pe_a1(i, dh):
            abanks[i, dh] = pe_s2(0, i, dh)

        def v_out2(i, part):
            on_pool = OMODE[i] == "B" or (OMODE[i] == "P" and part == 1)
            v_out(i, [slice(0, 512), slice(512, W), slice(0, W)][part], nc.gpsimd if on_pool else nc.vector)

        ops = dict(
            lu=load_u, lb=load_xb, lx=load_x, lw=load_wh, ls=load_s, lwe=load_we, lsm=load_small, ss=setup_s, sg=setup_g, sws=setup_we_scales, swc=setup_we_codes,
            m=v_m2, n=v_n2, t1=v_t1, t2=v_t2, sel=v_sel, T=pe_xt, xt=v_xt, qx=v_qx, S=pe_s1, th=a_tanh, g=v_g, qh=v_qh, gs=a_gs, H=pe_h, ch=a_ch, W=pe_w, cw=a_w, qw=v_qw,
            A=pe_a1, z=v_z, sig=a_sig, R=rec, dl=v_dl, sq=a_sq, ln=a_ln, mn=v_min, out=v_out2, so=store_out, RT=pe_rt, rc=cast_r, cr=a_rt, qr=v_qr, sc=store_codes, ssc=store_scales,
        )
        for step in ORDER:
            ops[step[0]](*step[1:])
